import numpy as np
import ml_dtypes


def mxq(x, axis, fmt="e4m3"):
    dtype, down = {"e4m3": (ml_dtypes.float8_e4m3fn, 7), "e5m2": (ml_dtypes.float8_e5m2, 14)}[fmt]
    v = np.moveaxis(np.asarray(x, np.float32).astype(ml_dtypes.bfloat16).astype(np.float64), axis, -1)
    blocks = v.reshape(v.shape[:-1] + (-1, 32))
    amax = np.abs(blocks).max(-1, keepdims=True)
    byte = np.maximum(np.where(amax > 0, np.frexp(amax)[1] - 1 + 127, 0) - down, 1)
    scale = np.exp2(byte - 127.0)
    codes = (blocks / scale).astype(np.float32).astype(dtype).astype(np.float64)
    return np.moveaxis((codes * scale).reshape(v.shape), -1, axis)


WIDE = False


def mx_kscale(k):
    if not WIDE:
        return np.ones(k)
    levels = np.array([10, -10, 5, -5, 0])
    if k % 512:
        return np.exp2(np.random.permutation(np.resize(levels, k // 32))).repeat(32)
    a = np.empty((k // 512, 16))
    for p in range(k // 512):
        a[p, :8] = np.random.permutation(np.resize(levels, 8))
        for g in range(8):
            far = levels[np.abs(levels - a[p, g]) >= 10]
            a[p, g + 8] = far[np.random.randint(len(far))]
    return np.exp2(a.ravel()).repeat(32)


def f64(x):
    return np.asarray(x).astype(np.float64)


def striped(idx):
    return np.tile(np.asarray(idx).reshape(-1, 16).T, (8, 1)).astype(np.uint16)


def unstriped(offs):
    return offs[:16].T.reshape(-1).astype(np.int64)


E2M1 = np.array([0.0, 0.5, 1.0, 1.5, 2.0, 3.0, 4.0, 6.0, -0.0, -0.5, -1.0, -1.5, -2.0, -3.0, -4.0, -6.0])


def pack_weight(w, fmt):
    k, n = w.shape
    w = f64(np.asarray(w, np.float32).astype(ml_dtypes.bfloat16)).reshape(k // 32, 32, n)
    amax = np.abs(w).max(1)
    if fmt == "e4m3":
        byte = np.frexp(amax)[1] - 1 + 127 - 7
    else:
        mant, ex = np.frexp(amax / 6.0)
        byte = np.where(mant > 0.5, ex, ex - 1) + 127
    byte = np.clip(np.where(amax > 0, byte, 1), 1, 254)
    scaled = (w * np.exp2(127.0 - byte)[:, None, :]).reshape(k, n).astype(np.float32)
    by_word = np.ascontiguousarray(scaled.reshape(k // 512, 128, 4, n).transpose(0, 1, 3, 2))
    if fmt == "e4m3":
        words = by_word.astype(ml_dtypes.float8_e4m3fn).view(np.uint8)
    else:
        c = by_word.astype(ml_dtypes.float4_e2m1fn).view(np.uint8) & 0xF
        words = (c[..., 0::2] | (c[..., 1::2] << 4)).reshape(k // 512, 128, 2 * n)
    return np.ascontiguousarray(words), np.ascontiguousarray(byte.astype(np.uint8).reshape(k // 512, 16, n))


def unpack_weight(words, scales, fmt):
    g, _, n = scales.shape
    words = np.ascontiguousarray(words).reshape(g, 128, n, -1)
    if fmt == "e4m3":
        vals = words.view(ml_dtypes.float8_e4m3fn).astype(np.float64)
    else:
        nib = np.empty((g, 128, n, 4), np.uint8)
        nib[..., 0::2] = words & 0xF
        nib[..., 1::2] = words >> 4
        vals = E2M1[nib]
    vals = vals * np.repeat(np.exp2(scales.astype(np.float64) - 127.0), 8, axis=1)[..., None]
    return vals.transpose(0, 1, 3, 2).reshape(g * 512, n)


def sigmoid(v):
    return 1.0 / (1.0 + np.exp(-v))


D, T, I, Q, G, E = 512, 2048, 512, 512, 128, 512


def setup_inputs():
    n = np.random.standard_normal
    idx = np.random.permutation(T)[:I]
    fd = mx_kscale(D)
    fi = mx_kscale(I)
    ti = np.ones(T)
    ti[idx] = fi
    keysp = pack_weight(n((D, T)) / fd[:, None], "e4m3")
    return {
        "query": (n((D, Q)) * 1.0 / np.sqrt(D) * fd[:, None]).astype(np.float32),
        "keys_words": keysp[0],
        "keys_scales": keysp[1],
        "steep": (np.random.uniform(1.0, 3.0, (I, 1))).astype(np.float32),
        "bias": (np.random.uniform(-2.0, 0.0, (I, 1))).astype(np.float32),
        "us": (np.random.uniform(0.02, 0.1, (I, 1)) * fi[:, None]).astype(np.float32),
        "vals": (n((E, T)) / ti).astype(np.float32),
        "offs": striped(idx),
    }


def reference(query, keys_words, keys_scales, steep, bias, us, vals, offs):
    idx = unstriped(offs)
    keysu = unpack_weight(keys_words, keys_scales, "e4m3")
    keysidxg = keysu[:, idx]
    queryq = mxq(f64(query), 0, "e4m3")
    a = keysidxg.T @ queryq
    s = a.reshape(I, G, Q // G).max(axis=2)
    w = sigmoid(s * f64(steep) + f64(bias)) * f64(us)
    vt = f64(vals)[:, idx].T
    wq = mxq(w, 0, "e4m3")
    vtq = mxq(vt, 0, "e4m3")
    o = wq.T @ vtq
    return o

@@ -1,0 +1,153 @@
+from contextlib import ExitStack
+
+import concourse.mybir as mybir
+from concourse.masks import make_identity
+
+D, T, I, Q, G, E = 512, 2048, 512, 512, 128, 512
+FLOPS = 2 * D * I * Q + 2 * I * G * E
+
+F32 = mybir.dt.float32
+BF16 = mybir.dt.bfloat16
+I32 = mybir.dt.int32
+U32 = mybir.dt.uint32
+U16 = mybir.dt.uint16
+U8 = mybir.dt.uint8
+FP8X4 = mybir.dt.float8_e4m3fn_x4
+ACT = mybir.ActivationFunctionType
+ALU = mybir.AluOpType
+
+P = 128
+PACK = 4
+BLOCKS = E // P
+QUERY_SPLIT = 352
+VECTOR_SLOTS = (0, 0, 256, 256)
+
+
+def tile_attend_anyquestion_kernel(tc, query, keys_words, keys_scales, steep, bias, us, vals, offs, out):
+    nc = tc.nc
+    with ExitStack() as ctx:
+        keep = ctx.enter_context(tc.tile_pool(name="keep", bufs=1))
+        psum = ctx.enter_context(tc.psum_pool(name="psum", bufs=1))
+
+        offsets = keep.tile([P, I // 16], U16, name="offsets")
+        q_raw = keep.tile([P, PACK, Q], F32, name="q_raw")
+        key_words = keep.tile([P, T], U32, name="key_words", align_bytes=64)
+        key_bytes = keep.tile([P, T], U8, name="key_bytes", align_bytes=64)
+        pools = [keep.tile([P, T], F32, name=f"pool{b}", align_bytes=64) for b in range(BLOCKS)]
+        steep_sb = keep.tile([P, PACK], F32, name="steep_sb")
+        bias_sb = keep.tile([P, PACK], F32, name="bias_sb")
+        us_sb = keep.tile([P, PACK], F32, name="us_sb")
+        identity = keep.tile([P, P], F32, name="identity")
+
+        nc.vector.memset(key_bytes[:].bitcast(I32), 0)
+
+        nc.sync.dma_start(out=q_raw[:], in_=query.rearrange("(p j) w -> p j w", j=PACK))
+        nc.sync.dma_start(offsets[:], offs)
+        for r in range(4):
+            nc.sync.dma_start(out=key_bytes[r:P:32, :].bitcast(I32), in_=keys_scales[0, r:16:4, :].bitcast(I32))
+        nc.sync.dma_start(
+            out=key_words[:].bitcast(I32), in_=keys_words[0].rearrange("p n t -> p (n t)").bitcast(I32)
+        )
+        for tile, vec in ((steep_sb, steep), (bias_sb, bias), (us_sb, us)):
+            nc.sync.dma_start(out=tile[:], in_=vec.rearrange("(p t) o -> p (t o)", t=PACK))
+        for b in range(BLOCKS):
+            nc.sync.dma_start(out=pools[b][:], in_=vals[b * P : (b + 1) * P, :])
+        make_identity(nc, identity[:])
+
+        q_grouped = keep.tile([P, Q, PACK], BF16, name="q_grouped", align_bytes=64)
+        for engine_copy, cols in (
+            (nc.vector.tensor_copy, slice(0, QUERY_SPLIT)),
+            (nc.scalar.copy, slice(QUERY_SPLIT, Q)),
+        ):
+            engine_copy(
+                out=q_grouped[:, cols, :].rearrange("p (c i) t -> p c t i", i=4),
+                in_=q_raw[:, :, cols].rearrange("p t (c i) -> p c t i", i=4),
+            )
+        q_codes = keep.tile([P, Q], U32, name="q_codes", align_bytes=64)
+        q_scales = keep.tile([P, Q], U8, name="q_scales", align_bytes=64)
+        nc.vector.quantize_mx(
+            out=q_codes[:].bitcast(FP8X4), scales=q_scales[:], in_=q_grouped[:].rearrange("p w t -> p (w t)")
+        )
+
+        k_scales = keep.tile([P, I], U8, name="k_scales", align_bytes=64)
+        k_codes = keep.tile([P, I], U32, name="k_codes", align_bytes=64)
+        nc.vector.tensor_copy(
+            out=k_scales[:].rearrange("p (t s) -> p s t", t=PACK), in_=key_bytes[:].indirect(offsets[:])
+        )
+        nc.vector.tensor_copy(
+            out=k_codes[:].rearrange("p (t s) -> p s t", t=PACK), in_=key_words[:].indirect(offsets[:])
+        )
+
+        best = keep.tile([P, PACK, G], F32, name="best")
+        gate = keep.tile([P, PACK, G], F32, name="gate")
+        for t in range(PACK):
+            cols = slice(t * P, (t + 1) * P)
+            scores = psum.tile([P, Q], F32, name=f"scores{t}")
+            nc.tensor.matmul_mx(
+                out=scores[:],
+                lhsT=k_codes[:, cols].bitcast(FP8X4),
+                lhsT_scale=k_scales[:, cols],
+                rhs=q_codes[:].bitcast(FP8X4),
+                rhs_scale=q_scales[:],
+                start=True,
+                stop=True,
+            )
+            nc.vector.tensor_reduce(
+                out=best[:, t, :],
+                in_=scores[:].rearrange("p (g j) -> p g j", j=Q // G),
+                axis=mybir.AxisListType.X,
+                op=ALU.max,
+            )
+            nc.scalar.activation(
+                out=gate[:, t, :],
+                in_=best[:, t, :],
+                func=ACT.Sigmoid,
+                bias=bias_sb[:, t : t + 1],
+                scale=steep_sb[:, t : t + 1],
+            )
+        w_grouped = keep.tile([P, G, PACK], BF16, name="w_grouped", align_bytes=64)
+        nc.vector.tensor_tensor(
+            out=w_grouped[:],
+            in0=gate[:].rearrange("p t g -> p g t"),
+            in1=us_sb[:].unsqueeze(1).to_broadcast([P, G, PACK]),
+            op=ALU.mult,
+        )
+        w_codes = keep.tile([P, G], U32, name="w_codes", align_bytes=64)
+        w_scales = keep.tile([P, G], U8, name="w_scales", align_bytes=64)
+        nc.vector.quantize_mx(
+            out=w_codes[:].bitcast(FP8X4), scales=w_scales[:], in_=w_grouped[:].rearrange("p g t -> p (g t)")
+        )
+
+        for b in range(BLOCKS):
+            listed = keep.tile([P, I], BF16, name=f"listed{b}", align_bytes=64)
+            split = VECTOR_SLOTS[b]
+            if split:
+                nc.vector.tensor_copy(out=listed[:, :split], in_=pools[b][:].indirect(offsets[:, : split // 16]))
+            nc.scalar.activation(
+                out=listed[:, split:], in_=pools[b][:].indirect(offsets[:, split // 16 :]), func=ACT.Copy
+            )
+            pairs = listed[:].bitcast(F32)
+            turned = psum.tile([P, 2, P], F32, name=f"turned{b % 2}")
+            for u in range(2):
+                nc.tensor.transpose(turned[:, u, :], pairs[:, u : I // 2 : 2], identity[:])
+            v_grouped = keep.tile([P, P * PACK], BF16, name=f"v_grouped{b}", align_bytes=64)
+            nc.scalar.copy(
+                out=v_grouped[:].bitcast(F32).rearrange("p (e u) -> p e u", u=2),
+                in_=turned[:].rearrange("p u e -> p e u"),
+            )
+            v_codes = keep.tile([P, P], U32, name=f"v_codes{b}", align_bytes=64)
+            v_scales = keep.tile([P, P], U8, name=f"v_scales{b}", align_bytes=64)
+            nc.vector.quantize_mx(out=v_codes[:].bitcast(FP8X4), scales=v_scales[:], in_=v_grouped[:])
+            sums = psum.tile([G, P], F32, name=f"sums{b % 2}")
+            nc.tensor.matmul_mx(
+                out=sums[:],
+                lhsT=w_codes[:].bitcast(FP8X4),
+                lhsT_scale=w_scales[:],
+                rhs=v_codes[:].bitcast(FP8X4),
+                rhs_scale=v_scales[:],
+                start=True,
+                stop=True,
+            )
+            result = keep.tile([G, P], F32, name=f"result{b}")
+            nc.scalar.copy(out=result[:], in_=sums[:])
+            nc.sync.dma_start(out=out[:, b * P : (b + 1) * P], in_=result[:])

@@ -20,7 +20,7 @@ P = 128
 PACK = 4
 BLOCKS = E // P
 QUERY_SPLIT = 352
-VECTOR_SLOTS = (0, 0, 256, 256)
+VECTOR_SLOTS = (0, 0, 288, 288)
 
 
 def tile_attend_anyquestion_kernel(tc, query, keys_words, keys_scales, steep, bias, us, vals, offs, out):
@@ -33,7 +33,7 @@ def tile_attend_anyquestion_kernel(tc, query, keys_words, keys_scales, steep, bi
         q_raw = keep.tile([P, PACK, Q], F32, name="q_raw")
         key_words = keep.tile([P, T], U32, name="key_words", align_bytes=64)
         key_bytes = keep.tile([P, T], U8, name="key_bytes", align_bytes=64)
-        pools = [keep.tile([P, T], F32, name=f"pool{b}", align_bytes=64) for b in range(BLOCKS)]
+        pools = [keep.tile([P, T], F32, name=f"pool{b}", tag=f"pool{b}", align_bytes=64) for b in range(BLOCKS)]
         steep_sb = keep.tile([P, PACK], F32, name="steep_sb")
         bias_sb = keep.tile([P, PACK], F32, name="bias_sb")
         us_sb = keep.tile([P, PACK], F32, name="us_sb")
@@ -48,9 +48,10 @@ def tile_attend_anyquestion_kernel(tc, query, keys_words, keys_scales, steep, bi
         nc.sync.dma_start(
             out=key_words[:].bitcast(I32), in_=keys_words[0].rearrange("p n t -> p (n t)").bitcast(I32)
         )
+        nc.sync.dma_start(out=pools[0][:], in_=vals[:P, :])
         for tile, vec in ((steep_sb, steep), (bias_sb, bias), (us_sb, us)):
             nc.sync.dma_start(out=tile[:], in_=vec.rearrange("(p t) o -> p (t o)", t=PACK))
-        for b in range(BLOCKS):
+        for b in range(1, BLOCKS):
             nc.sync.dma_start(out=pools[b][:], in_=vals[b * P : (b + 1) * P, :])
         make_identity(nc, identity[:])
 
@@ -118,7 +119,11 @@ def tile_attend_anyquestion_kernel(tc, query, keys_words, keys_scales, steep, bi
             out=w_codes[:].bitcast(FP8X4), scales=w_scales[:], in_=w_grouped[:].rearrange("p g t -> p (g t)")
         )
 
-        for b in range(BLOCKS):
+        v_codes = keep.tile([P, E], U32, name="v_codes", align_bytes=64)
+        v_scales = keep.tile([P, E], U8, name="v_scales", align_bytes=64)
+        sums = [psum.tile([G, E // 2], F32, name=f"sums{h}") for h in range(2)]
+
+        def turn(b):
             listed = keep.tile([P, I], BF16, name=f"listed{b}", align_bytes=64)
             split = VECTOR_SLOTS[b]
             if split:
@@ -127,27 +132,42 @@ def tile_attend_anyquestion_kernel(tc, query, keys_words, keys_scales, steep, bi
                 out=listed[:, split:], in_=pools[b][:].indirect(offsets[:, split // 16 :]), func=ACT.Copy
             )
             pairs = listed[:].bitcast(F32)
-            turned = psum.tile([P, 2, P], F32, name=f"turned{b % 2}")
+            turned = psum.tile([P, 2, P], F32, name=f"turned{b}", tag=("turned0", "turned1", "scores0", "scores1")[b])
             for u in range(2):
                 nc.tensor.transpose(turned[:, u, :], pairs[:, u : I // 2 : 2], identity[:])
-            v_grouped = keep.tile([P, P * PACK], BF16, name=f"v_grouped{b}", align_bytes=64)
-            nc.scalar.copy(
-                out=v_grouped[:].bitcast(F32).rearrange("p (e u) -> p e u", u=2),
-                in_=turned[:].rearrange("p u e -> p e u"),
-            )
-            v_codes = keep.tile([P, P], U32, name=f"v_codes{b}", align_bytes=64)
-            v_scales = keep.tile([P, P], U8, name=f"v_scales{b}", align_bytes=64)
-            nc.vector.quantize_mx(out=v_codes[:].bitcast(FP8X4), scales=v_scales[:], in_=v_grouped[:])
-            sums = psum.tile([G, P], F32, name=f"sums{b % 2}")
+            return turned
+
+        def interleave(copy, turned, grouped):
+            copy(out=grouped.rearrange("p (e u) -> p e u", u=2), in_=turned[:].rearrange("p u e -> p e u"))
+
+        def multiply(first, last, grouped):
+            cols = slice(first * P, last * P)
+            nc.vector.quantize_mx(out=v_codes[:, cols].bitcast(FP8X4), scales=v_scales[:, cols], in_=grouped.bitcast(BF16))
+            half = first // 2
             nc.tensor.matmul_mx(
-                out=sums[:],
+                out=sums[half][:, (first - 2 * half) * P : (last - 2 * half) * P],
                 lhsT=w_codes[:].bitcast(FP8X4),
                 lhsT_scale=w_scales[:],
-                rhs=v_codes[:].bitcast(FP8X4),
-                rhs_scale=v_scales[:],
+                rhs=v_codes[:, cols].bitcast(FP8X4),
+                rhs_scale=v_scales[:, cols],
                 start=True,
                 stop=True,
             )
-            result = keep.tile([G, P], F32, name=f"result{b}")
-            nc.scalar.copy(out=result[:], in_=sums[:])
-            nc.sync.dma_start(out=out[:, b * P : (b + 1) * P], in_=result[:])
+
+        W = 2 * P
+        turned = [turn(0), turn(1), turn(2)]
+        front = keep.tile([P, 2 * W], F32, name="front", tag="pool2", align_bytes=64)
+        interleave(nc.vector.tensor_copy, turned[0], front[:, :W])
+        interleave(nc.scalar.copy, turned[1], front[:, W:])
+        multiply(0, 2, front[:])
+        turned.append(turn(3))
+        back = keep.tile([P, 3 * W], F32, name="back", tag="pool3", align_bytes=64)
+        nc.vector.tensor_copy(out=back[:, 2 * W :], in_=sums[0][:])
+        nc.sync.dma_start(out=out[:, : E // 2], in_=back[:, 2 * W :])
+        for b in (2, 3):
+            grouped = back[:, (b - 2) * W : (b - 1) * W]
+            interleave(nc.scalar.copy, turned[b], grouped)
+            multiply(b, b + 1, grouped)
+        late = keep.tile([G, E // 2], F32, name="late")
+        nc.scalar.copy(out=late[:], in_=sums[1][:])
+        nc.sync.dma_start(out=out[:, E // 2 :], in_=late[:])

@@ -20,20 +20,22 @@ P = 128
 PACK = 4
 BLOCKS = E // P
 QUERY_SPLIT = 352
-VECTOR_SLOTS = (0, 0, 288, 288)
+VECTOR_SLOTS = (0, 0, 320, 288)
 
 
 def tile_attend_anyquestion_kernel(tc, query, keys_words, keys_scales, steep, bias, us, vals, offs, out):
     nc = tc.nc
     with ExitStack() as ctx:
         keep = ctx.enter_context(tc.tile_pool(name="keep", bufs=1))
+        shared = ctx.enter_context(tc.tile_pool(name="shared", bufs=1))
         psum = ctx.enter_context(tc.psum_pool(name="psum", bufs=1))
 
         offsets = keep.tile([P, I // 16], U16, name="offsets")
         q_raw = keep.tile([P, PACK, Q], F32, name="q_raw")
         key_words = keep.tile([P, T], U32, name="key_words", align_bytes=64)
         key_bytes = keep.tile([P, T], U8, name="key_bytes", align_bytes=64)
-        pools = [keep.tile([P, T], F32, name=f"pool{b}", tag=f"pool{b}", align_bytes=64) for b in range(BLOCKS)]
+        pools = [keep.tile([P, T], F32, name=f"pool{b}", tag=f"pool{b}", align_bytes=64) for b in range(BLOCKS - 1)]
+        pools.append(shared.tile([P, T], F32, name="pool3", align_bytes=64, offset=0))
         steep_sb = keep.tile([P, PACK], F32, name="steep_sb")
         bias_sb = keep.tile([P, PACK], F32, name="bias_sb")
         us_sb = keep.tile([P, PACK], F32, name="us_sb")
@@ -108,9 +110,9 @@ def tile_attend_anyquestion_kernel(tc, query, keys_words, keys_scales, steep, bi
             )
         w_grouped = keep.tile([P, G, PACK], BF16, name="w_grouped", align_bytes=64)
         nc.vector.tensor_tensor(
-            out=w_grouped[:],
-            in0=gate[:].rearrange("p t g -> p g t"),
-            in1=us_sb[:].unsqueeze(1).to_broadcast([P, G, PACK]),
+            out=w_grouped[:].rearrange("p (c i) t -> p c t i", i=4),
+            in0=gate[:].rearrange("p t (c i) -> p c t i", i=4),
+            in1=us_sb[:].unsqueeze(1).unsqueeze(3).to_broadcast([P, G // 4, PACK, 4]),
             op=ALU.mult,
         )
         w_codes = keep.tile([P, G], U32, name="w_codes", align_bytes=64)
@@ -118,10 +120,6 @@ def tile_attend_anyquestion_kernel(tc, query, keys_words, keys_scales, steep, bi
         nc.vector.quantize_mx(
             out=w_codes[:].bitcast(FP8X4), scales=w_scales[:], in_=w_grouped[:].rearrange("p g t -> p (g t)")
         )
-
-        v_codes = keep.tile([P, E], U32, name="v_codes", align_bytes=64)
-        v_scales = keep.tile([P, E], U8, name="v_scales", align_bytes=64)
-        sums = [psum.tile([G, E // 2], F32, name=f"sums{h}") for h in range(2)]
 
         def turn(b):
             listed = keep.tile([P, I], BF16, name=f"listed{b}", align_bytes=64)
@@ -140,34 +138,37 @@ def tile_attend_anyquestion_kernel(tc, query, keys_words, keys_scales, steep, bi
         def interleave(copy, turned, grouped):
             copy(out=grouped.rearrange("p (e u) -> p e u", u=2), in_=turned[:].rearrange("p u e -> p e u"))
 
-        def multiply(first, last, grouped):
-            cols = slice(first * P, last * P)
-            nc.vector.quantize_mx(out=v_codes[:, cols].bitcast(FP8X4), scales=v_scales[:, cols], in_=grouped.bitcast(BF16))
-            half = first // 2
+        def multiply(grouped, codes, scales, sums):
+            nc.vector.quantize_mx(out=codes.bitcast(FP8X4), scales=scales, in_=grouped.bitcast(BF16))
             nc.tensor.matmul_mx(
-                out=sums[half][:, (first - 2 * half) * P : (last - 2 * half) * P],
+                out=sums,
                 lhsT=w_codes[:].bitcast(FP8X4),
                 lhsT_scale=w_scales[:],
-                rhs=v_codes[:, cols].bitcast(FP8X4),
-                rhs_scale=v_scales[:, cols],
+                rhs=codes.bitcast(FP8X4),
+                rhs_scale=scales,
                 start=True,
                 stop=True,
             )
 
         W = 2 * P
+        early_sums = psum.tile([G, 3 * P], F32, name="early_sums")
+        last_sums = psum.tile([G, P], F32, name="last_sums")
         turned = [turn(0), turn(1), turn(2)]
         front = keep.tile([P, 2 * W], F32, name="front", tag="pool2", align_bytes=64)
         interleave(nc.vector.tensor_copy, turned[0], front[:, :W])
         interleave(nc.scalar.copy, turned[1], front[:, W:])
-        multiply(0, 2, front[:])
         turned.append(turn(3))
-        back = keep.tile([P, 3 * W], F32, name="back", tag="pool3", align_bytes=64)
-        nc.vector.tensor_copy(out=back[:, 2 * W :], in_=sums[0][:])
-        nc.sync.dma_start(out=out[:, : E // 2], in_=back[:, 2 * W :])
-        for b in (2, 3):
+        v_codes = shared.tile([P, E], U32, name="v_codes", align_bytes=64, offset=0)
+        v_scales = keep.tile([P, E], U8, name="v_scales", align_bytes=64)
+        back = shared.tile([P, 2 * W], F32, name="back", align_bytes=64, offset=4 * E)
+        multiply(front[:], v_codes[:, : 2 * P], v_scales[:, : 2 * P], early_sums[:, : 2 * P])
+        for b, sums in ((2, early_sums[:, 2 * P :]), (3, last_sums[:])):
             grouped = back[:, (b - 2) * W : (b - 1) * W]
             interleave(nc.scalar.copy, turned[b], grouped)
-            multiply(b, b + 1, grouped)
-        late = keep.tile([G, E // 2], F32, name="late")
-        nc.scalar.copy(out=late[:], in_=sums[1][:])
-        nc.sync.dma_start(out=out[:, E // 2 :], in_=late[:])
+            multiply(grouped, v_codes[:, b * P : (b + 1) * P], v_scales[:, b * P : (b + 1) * P], sums)
+        early = keep.tile([G, 3 * P], F32, name="early")
+        nc.scalar.copy(out=early[:], in_=early_sums[:])
+        nc.sync.dma_start(out=out[:, : 3 * P], in_=early[:])
+        late = keep.tile([G, P], F32, name="late")
+        nc.vector.tensor_copy(out=late[:], in_=last_sums[:])
+        nc.sync.dma_start(out=out[:, 3 * P :], in_=late[:])

@@ -20,7 +20,7 @@ P = 128
 PACK = 4
 BLOCKS = E // P
 QUERY_SPLIT = 352
-VECTOR_SLOTS = (0, 0, 320, 288)
+VECTOR_SLOTS = (0, 0, 224, 288)
 
 
 def tile_attend_anyquestion_kernel(tc, query, keys_words, keys_scales, steep, bias, us, vals, offs, out):

from contextlib import ExitStack

import concourse.mybir as mybir
from concourse.masks import make_identity

D, T, I, Q, G, E = 512, 2048, 512, 512, 128, 512
FLOPS = 2 * D * I * Q + 2 * I * G * E

F32 = mybir.dt.float32
BF16 = mybir.dt.bfloat16
I32 = mybir.dt.int32
U32 = mybir.dt.uint32
U16 = mybir.dt.uint16
U8 = mybir.dt.uint8
FP8X4 = mybir.dt.float8_e4m3fn_x4
ACT = mybir.ActivationFunctionType
ALU = mybir.AluOpType

P = 128
PACK = 4
BLOCKS = E // P
QUERY_SPLIT = 352
VECTOR_SLOTS = (0, 0, 224, 288)


def tile_attend_anyquestion_kernel(tc, query, keys_words, keys_scales, steep, bias, us, vals, offs, out):
    nc = tc.nc
    with ExitStack() as ctx:
        keep = ctx.enter_context(tc.tile_pool(name="keep", bufs=1))
        shared = ctx.enter_context(tc.tile_pool(name="shared", bufs=1))
        psum = ctx.enter_context(tc.psum_pool(name="psum", bufs=1))

        offsets = keep.tile([P, I // 16], U16, name="offsets")
        q_raw = keep.tile([P, PACK, Q], F32, name="q_raw")
        key_words = keep.tile([P, T], U32, name="key_words", align_bytes=64)
        key_bytes = keep.tile([P, T], U8, name="key_bytes", align_bytes=64)
        pools = [keep.tile([P, T], F32, name=f"pool{b}", tag=f"pool{b}", align_bytes=64) for b in range(BLOCKS - 1)]
        pools.append(shared.tile([P, T], F32, name="pool3", align_bytes=64, offset=0))
        steep_sb = keep.tile([P, PACK], F32, name="steep_sb")
        bias_sb = keep.tile([P, PACK], F32, name="bias_sb")
        us_sb = keep.tile([P, PACK], F32, name="us_sb")
        identity = keep.tile([P, P], F32, name="identity")

        nc.vector.memset(key_bytes[:].bitcast(I32), 0)

        nc.sync.dma_start(out=q_raw[:], in_=query.rearrange("(p j) w -> p j w", j=PACK))
        nc.sync.dma_start(offsets[:], offs)
        for r in range(4):
            nc.sync.dma_start(out=key_bytes[r:P:32, :].bitcast(I32), in_=keys_scales[0, r:16:4, :].bitcast(I32))
        nc.sync.dma_start(
            out=key_words[:].bitcast(I32), in_=keys_words[0].rearrange("p n t -> p (n t)").bitcast(I32)
        )
        nc.sync.dma_start(out=pools[0][:], in_=vals[:P, :])
        for tile, vec in ((steep_sb, steep), (bias_sb, bias), (us_sb, us)):
            nc.sync.dma_start(out=tile[:], in_=vec.rearrange("(p t) o -> p (t o)", t=PACK))
        for b in range(1, BLOCKS):
            nc.sync.dma_start(out=pools[b][:], in_=vals[b * P : (b + 1) * P, :])
        make_identity(nc, identity[:])

        q_grouped = keep.tile([P, Q, PACK], BF16, name="q_grouped", align_bytes=64)
        for engine_copy, cols in (
            (nc.vector.tensor_copy, slice(0, QUERY_SPLIT)),
            (nc.scalar.copy, slice(QUERY_SPLIT, Q)),
        ):
            engine_copy(
                out=q_grouped[:, cols, :].rearrange("p (c i) t -> p c t i", i=4),
                in_=q_raw[:, :, cols].rearrange("p t (c i) -> p c t i", i=4),
            )
        q_codes = keep.tile([P, Q], U32, name="q_codes", align_bytes=64)
        q_scales = keep.tile([P, Q], U8, name="q_scales", align_bytes=64)
        nc.vector.quantize_mx(
            out=q_codes[:].bitcast(FP8X4), scales=q_scales[:], in_=q_grouped[:].rearrange("p w t -> p (w t)")
        )

        k_scales = keep.tile([P, I], U8, name="k_scales", align_bytes=64)
        k_codes = keep.tile([P, I], U32, name="k_codes", align_bytes=64)
        nc.vector.tensor_copy(
            out=k_scales[:].rearrange("p (t s) -> p s t", t=PACK), in_=key_bytes[:].indirect(offsets[:])
        )
        nc.vector.tensor_copy(
            out=k_codes[:].rearrange("p (t s) -> p s t", t=PACK), in_=key_words[:].indirect(offsets[:])
        )

        best = keep.tile([P, PACK, G], F32, name="best")
        gate = keep.tile([P, PACK, G], F32, name="gate")
        for t in range(PACK):
            cols = slice(t * P, (t + 1) * P)
            scores = psum.tile([P, Q], F32, name=f"scores{t}")
            nc.tensor.matmul_mx(
                out=scores[:],
                lhsT=k_codes[:, cols].bitcast(FP8X4),
                lhsT_scale=k_scales[:, cols],
                rhs=q_codes[:].bitcast(FP8X4),
                rhs_scale=q_scales[:],
                start=True,
                stop=True,
            )
            nc.vector.tensor_reduce(
                out=best[:, t, :],
                in_=scores[:].rearrange("p (g j) -> p g j", j=Q // G),
                axis=mybir.AxisListType.X,
                op=ALU.max,
            )
            nc.scalar.activation(
                out=gate[:, t, :],
                in_=best[:, t, :],
                func=ACT.Sigmoid,
                bias=bias_sb[:, t : t + 1],
                scale=steep_sb[:, t : t + 1],
            )
        w_grouped = keep.tile([P, G, PACK], BF16, name="w_grouped", align_bytes=64)
        nc.vector.tensor_tensor(
            out=w_grouped[:].rearrange("p (c i) t -> p c t i", i=4),
            in0=gate[:].rearrange("p t (c i) -> p c t i", i=4),
            in1=us_sb[:].unsqueeze(1).unsqueeze(3).to_broadcast([P, G // 4, PACK, 4]),
            op=ALU.mult,
        )
        w_codes = keep.tile([P, G], U32, name="w_codes", align_bytes=64)
        w_scales = keep.tile([P, G], U8, name="w_scales", align_bytes=64)
        nc.vector.quantize_mx(
            out=w_codes[:].bitcast(FP8X4), scales=w_scales[:], in_=w_grouped[:].rearrange("p g t -> p (g t)")
        )

        def turn(b):
            listed = keep.tile([P, I], BF16, name=f"listed{b}", align_bytes=64)
            split = VECTOR_SLOTS[b]
            if split:
                nc.vector.tensor_copy(out=listed[:, :split], in_=pools[b][:].indirect(offsets[:, : split // 16]))
            nc.scalar.activation(
                out=listed[:, split:], in_=pools[b][:].indirect(offsets[:, split // 16 :]), func=ACT.Copy
            )
            pairs = listed[:].bitcast(F32)
            turned = psum.tile([P, 2, P], F32, name=f"turned{b}", tag=("turned0", "turned1", "scores0", "scores1")[b])
            for u in range(2):
                nc.tensor.transpose(turned[:, u, :], pairs[:, u : I // 2 : 2], identity[:])
            return turned

        def interleave(copy, turned, grouped):
            copy(out=grouped.rearrange("p (e u) -> p e u", u=2), in_=turned[:].rearrange("p u e -> p e u"))

        def multiply(grouped, codes, scales, sums):
            nc.vector.quantize_mx(out=codes.bitcast(FP8X4), scales=scales, in_=grouped.bitcast(BF16))
            nc.tensor.matmul_mx(
                out=sums,
                lhsT=w_codes[:].bitcast(FP8X4),
                lhsT_scale=w_scales[:],
                rhs=codes.bitcast(FP8X4),
                rhs_scale=scales,
                start=True,
                stop=True,
            )

        W = 2 * P
        early_sums = psum.tile([G, 3 * P], F32, name="early_sums")
        last_sums = psum.tile([G, P], F32, name="last_sums")
        turned = [turn(0), turn(1), turn(2)]
        front = keep.tile([P, 2 * W], F32, name="front", tag="pool2", align_bytes=64)
        interleave(nc.vector.tensor_copy, turned[0], front[:, :W])
        interleave(nc.scalar.copy, turned[1], front[:, W:])
        turned.append(turn(3))
        v_codes = shared.tile([P, E], U32, name="v_codes", align_bytes=64, offset=0)
        v_scales = keep.tile([P, E], U8, name="v_scales", align_bytes=64)
        back = shared.tile([P, 2 * W], F32, name="back", align_bytes=64, offset=4 * E)
        multiply(front[:], v_codes[:, : 2 * P], v_scales[:, : 2 * P], early_sums[:, : 2 * P])
        for b, sums in ((2, early_sums[:, 2 * P :]), (3, last_sums[:])):
            grouped = back[:, (b - 2) * W : (b - 1) * W]
            interleave(nc.scalar.copy, turned[b], grouped)
            multiply(grouped, v_codes[:, b * P : (b + 1) * P], v_scales[:, b * P : (b + 1) * P], sums)
        early = keep.tile([G, 3 * P], F32, name="early")
        nc.scalar.copy(out=early[:], in_=early_sums[:])
        nc.sync.dma_start(out=out[:, : 3 * P], in_=early[:])
        late = keep.tile([G, P], F32, name="late")
        nc.vector.tensor_copy(out=late[:], in_=last_sums[:])
        nc.sync.dma_start(out=out[:, 3 * P :], in_=late[:])
